import numpy as np
import ml_dtypes


def mxq(x, axis, fmt="e4m3"):
    dtype, down = {"e4m3": (ml_dtypes.float8_e4m3fn, 7), "e5m2": (ml_dtypes.float8_e5m2, 14)}[fmt]
    v = np.moveaxis(np.asarray(x, np.float32).astype(ml_dtypes.bfloat16).astype(np.float64), axis, -1)
    blocks = v.reshape(v.shape[:-1] + (-1, 32))
    amax = np.abs(blocks).max(-1, keepdims=True)
    byte = np.maximum(np.where(amax > 0, np.frexp(amax)[1] - 1 + 127, 0) - down, 1)
    scale = np.exp2(byte - 127.0)
    codes = (blocks / scale).astype(np.float32).astype(dtype).astype(np.float64)
    return np.moveaxis((codes * scale).reshape(v.shape), -1, axis)


WIDE = False


def mx_kscale(k):
    if not WIDE:
        return np.ones(k)
    levels = np.array([10, -10, 5, -5, 0])
    if k % 512:
        return np.exp2(np.random.permutation(np.resize(levels, k // 32))).repeat(32)
    a = np.empty((k // 512, 16))
    for p in range(k // 512):
        a[p, :8] = np.random.permutation(np.resize(levels, 8))
        for g in range(8):
            far = levels[np.abs(levels - a[p, g]) >= 10]
            a[p, g + 8] = far[np.random.randint(len(far))]
    return np.exp2(a.ravel()).repeat(32)


def f64(x):
    return np.asarray(x).astype(np.float64)


def striped(idx):
    return np.tile(np.asarray(idx).reshape(-1, 16).T, (8, 1)).astype(np.uint16)


def unstriped(offs):
    return offs[:16].T.reshape(-1).astype(np.int64)


E2M1 = np.array([0.0, 0.5, 1.0, 1.5, 2.0, 3.0, 4.0, 6.0, -0.0, -0.5, -1.0, -1.5, -2.0, -3.0, -4.0, -6.0])


def pack_weight(w, fmt):
    k, n = w.shape
    w = f64(np.asarray(w, np.float32).astype(ml_dtypes.bfloat16)).reshape(k // 32, 32, n)
    amax = np.abs(w).max(1)
    if fmt == "e4m3":
        byte = np.frexp(amax)[1] - 1 + 127 - 7
    else:
        mant, ex = np.frexp(amax / 6.0)
        byte = np.where(mant > 0.5, ex, ex - 1) + 127
    byte = np.clip(np.where(amax > 0, byte, 1), 1, 254)
    scaled = (w * np.exp2(127.0 - byte)[:, None, :]).reshape(k, n).astype(np.float32)
    by_word = np.ascontiguousarray(scaled.reshape(k // 512, 128, 4, n).transpose(0, 1, 3, 2))
    if fmt == "e4m3":
        words = by_word.astype(ml_dtypes.float8_e4m3fn).view(np.uint8)
    else:
        c = by_word.astype(ml_dtypes.float4_e2m1fn).view(np.uint8) & 0xF
        words = (c[..., 0::2] | (c[..., 1::2] << 4)).reshape(k // 512, 128, 2 * n)
    return np.ascontiguousarray(words), np.ascontiguousarray(byte.astype(np.uint8).reshape(k // 512, 16, n))


def unpack_weight(words, scales, fmt):
    g, _, n = scales.shape
    words = np.ascontiguousarray(words).reshape(g, 128, n, -1)
    if fmt == "e4m3":
        vals = words.view(ml_dtypes.float8_e4m3fn).astype(np.float64)
    else:
        nib = np.empty((g, 128, n, 4), np.uint8)
        nib[..., 0::2] = words & 0xF
        nib[..., 1::2] = words >> 4
        vals = E2M1[nib]
    vals = vals * np.repeat(np.exp2(scales.astype(np.float64) - 127.0), 8, axis=1)[..., None]
    return vals.transpose(0, 1, 3, 2).reshape(g * 512, n)


def sigmoid(v):
    return 1.0 / (1.0 + np.exp(-v))


D, E, T, I, Q = 512, 512, 2048, 512, 128


def setup_inputs():
    n = np.random.standard_normal
    idx = np.random.permutation(T)[:I]
    fd = mx_kscale(D)
    fe = mx_kscale(E)
    keysp = pack_weight(n((D, T)) / fd[:, None], "e2m1")
    valsp = pack_weight(n((E, T)) / fe[:, None], "e2m1")
    return {
        "query": (n((D, Q)) * 0.6 / np.sqrt(D) * fd[:, None]).astype(np.float32),
        "keys_words": keysp[0],
        "keys_scales": keysp[1],
        "th": (np.random.uniform(5.8, 6.8, (Q, 1))).astype(np.float32),
        "steep": (np.random.uniform(1.0, 4.0, (Q, 1))).astype(np.float32),
        "kdot": (np.random.uniform(-1.0, 1.0, (Q, 1))).astype(np.float32),
        "gout": (n((E, Q)) * 1 / np.sqrt(E) * fe[:, None]).astype(np.float32),
        "vals_words": valsp[0],
        "vals_scales": valsp[1],
        "old": (0.5 * n((Q, T))).astype(np.float32),
        "offs": striped(idx),
    }


def reference(query, keys_words, keys_scales, th, steep, kdot, gout, vals_words, vals_scales, old, offs):
    idx = unstriped(offs)
    keysu = unpack_weight(keys_words, keys_scales, "e2m1")
    valsu = unpack_weight(vals_words, vals_scales, "e2m1")
    queryq = mxq(f64(query), 0, "e4m3")
    keysidxg = keysu[:, idx]
    a = queryq.T @ keysidxg
    p = np.exp(a)
    z = np.sum(p, axis=1, keepdims=True)
    gt = sigmoid((np.log(z) - f64(th)) * f64(steep))
    goutq = mxq(f64(gout), 0, "e4m3")
    valsidxg = valsu[:, idx]
    c0 = goutq.T @ valsidxg
    dgt = np.sum(p * c0, axis=1, keepdims=True) / z - f64(kdot)
    dz = dgt * gt * (1.0 - gt) * f64(steep) / z - gt * np.sum(p * c0, axis=1, keepdims=True) / np.square(z)
    dp = gt / z * c0 + dz
    da = dp * p
    gs = da * 1024.0
    gf = np.zeros((Q, T))
    gf[:, idx] = gs
    y = f64(old) + gf
    return y

@@ -1,0 +1,149 @@
+from contextlib import ExitStack
+
+import concourse.mybir as mybir
+
+D, T, I, Q = 512, 2048, 512, 128
+FLOPS = 2 * 2 * D * I * Q
+
+F32 = mybir.dt.float32
+BF16 = mybir.dt.bfloat16
+I32 = mybir.dt.int32
+U32 = mybir.dt.uint32
+U16 = mybir.dt.uint16
+U8 = mybir.dt.uint8
+FP8X4 = mybir.dt.float8_e4m3fn_x4
+FP4X4 = mybir.dt.float4_e2m1fn_x4
+ALU = mybir.AluOpType
+ACT = mybir.ActivationFunctionType
+
+P = 128
+PACK = 4
+HALF = I // 2
+GRAD_SCALE = 1024.0
+SPAN = 32.0
+CHUNKS = [128,384,512,512,512]
+
+
+def tile_attend_bupdategate_s_kernel(tc, query, keys_words, keys_scales, th, steep, kdot, gout, vals_words, vals_scales, old, offs, out):
+    nc = tc.nc
+    with ExitStack() as ctx:
+        sb = ctx.enter_context(tc.tile_pool(name="sb", bufs=1))
+        ps = ctx.enter_context(tc.psum_pool(name="ps", bufs=1))
+
+        def col(name, width=1, tag=""):
+            return sb.tile([P, width], F32, name=name, tag=tag)
+
+        offsets = sb.tile([P, I // 16], U16, name="offsets")
+        halves = [slice(h * HALF, (h + 1) * HALF) for h in range(2)]
+        half_offsets = [offsets[:, h * (HALF // 16) : (h + 1) * (HALF // 16)] for h in range(2)]
+        k_words = sb.tile([P, T], U16, name="k_words")
+        k_bytes = sb.tile([P, T], U8, name="k_bytes", tag="slot_a")
+        v_bytes = sb.tile([P, T], U8, name="v_bytes", tag="slot_b")
+        q_raw = sb.tile([P, PACK, Q], F32, name="q_raw", tag="slot_c")
+        g_raw = sb.tile([P, PACK, Q], F32, name="g_raw")
+        th_c, steep_c, kdot_c = col("th_c"), col("steep_c"), col("kdot_c")
+        placed = sb.tile([P, T], F32, name="placed")
+        warm_in, warm_out = col("warm_in"), col("warm_out")
+
+        nc.vector.memset(k_bytes[:].bitcast(I32), 0)
+        nc.vector.memset(warm_in[:], 0.0)
+        nc.vector.memset(placed[:], 0.0)
+        nc.vector.memset(v_bytes[:].bitcast(I32), 0)
+
+        def load_bytes(queue, tile, scales):
+            for quad in range(4):
+                queue.dma_start(tile[32 * quad : 32 * quad + 4, :].bitcast(I32), scales[0, 4 * quad : 4 * quad + 4, :].bitcast(I32))
+
+        nc.sync.dma_start(offsets[:], offs)
+        nc.sync.dma_start(k_words[:].bitcast(I32), keys_words[0].bitcast(I32))
+        nc.sync.dma_start(q_raw[:], query.rearrange("(p j) w -> p j w", j=PACK))
+        load_bytes(nc.scalar, k_bytes, keys_scales)
+        nc.scalar.activation(warm_out[:], warm_in[:], ACT.Exp)
+        nc.sync.dma_start(g_raw[:], gout.rearrange("(p j) w -> p j w", j=PACK))
+        nc.gpsimd.dma_start(th_c[:], th)
+        nc.gpsimd.dma_start(steep_c[:], steep)
+        nc.gpsimd.dma_start(kdot_c[:], kdot)
+        load_bytes(nc.sync, v_bytes, vals_scales)
+
+        def quantise(raw, name):
+            woven = sb.tile([P, Q, PACK], BF16, name=name + "_woven", align_bytes=64)
+            codes = sb.tile([P, Q], U32, name=name + "_codes", align_bytes=64)
+            plane = sb.tile([P, Q], U8, name=name + "_plane", align_bytes=64)
+            nc.scalar.copy(woven[:], raw[:].rearrange("p j w -> p w j"))
+            nc.vector.quantize_mx(out=codes[:].bitcast(FP8X4), scales=plane[:], in_=woven[:].rearrange("p w j -> p (w j)"))
+            return codes, plane
+
+        def product(bank, codes, plane, words, scale_bytes):
+            nc.tensor.matmul_mx(out=bank, lhsT=codes[:].bitcast(FP8X4), lhsT_scale=plane[:],
+                                rhs=words.bitcast(FP4X4), rhs_scale=scale_bytes, start=True, stop=True)
+
+        k_picked = sb.tile([P, I], U16, name="k_picked", tag="picked_words", align_bytes=64)
+        k_scale = sb.tile([P, I], U8, name="k_scale", tag="picked_bytes", align_bytes=64)
+        nc.vector.tensor_copy(k_picked[:], k_words[:].indirect(offsets[:]))
+        q_codes, q_plane = quantise(q_raw, "q")
+        v_words = sb.tile([P, T], U16, name="v_words", tag="slot_c")
+        nc.sync.dma_start(v_words[:].bitcast(I32), vals_words[0].bitcast(I32))
+        g_codes, g_plane = quantise(g_raw, "g")
+        a_banks = [ps.tile([P, HALF], F32, name="a_bank%d" % h) for h in range(2)]
+        for h in range(2):
+            nc.vector.tensor_copy(k_scale[:, halves[h]], k_bytes[:].indirect(half_offsets[h]))
+            product(a_banks[h][:], q_codes, q_plane, k_picked[:, halves[h]], k_scale[:, halves[h]])
+        old_lo = sb.tile([P, T // 2], F32, name="old_lo", tag="slot_a")
+        nc.sync.dma_start(old_lo[:], old[:, 0 : T // 2])
+        neg_a = sb.tile([P, I], F32, name="neg_a")
+        neg_max_first, neg_max = col("neg_max_first"), col("neg_max")
+        nc.vector.tensor_scalar(neg_a[:, halves[0]], a_banks[0][:], -1.0, None, ALU.mult, ALU.min, accum_out=neg_max_first[:])
+        nc.vector.tensor_scalar(neg_a[:, halves[1]], a_banks[1][:], -1.0, neg_max_first[:], ALU.mult, ALU.min, accum_out=neg_max[:])
+
+        th_unit, steep_th, neg_steep, steep_less_one, neg_span_steep = [col(n) for n in ("th_unit", "steep_th", "neg_steep", "steep_less_one", "neg_span_steep")]
+        nc.gpsimd.tensor_scalar(th_unit[:], th_c[:], 1.0 / SPAN, 0.0, ALU.mult, ALU.add)
+        nc.gpsimd.tensor_scalar(steep_th[:], th_c[:], steep_c[:], 1.0, ALU.mult, ALU.mult)
+        nc.gpsimd.tensor_scalar(neg_span_steep[:], steep_c[:], -SPAN, 0.0, ALU.mult, ALU.add)
+        nc.gpsimd.tensor_scalar(neg_steep[:], steep_c[:], -1.0, 0.0, ALU.mult, ALU.add)
+        nc.gpsimd.tensor_scalar(steep_less_one[:], steep_c[:], 1.0, -1.0, ALU.mult, ALU.add)
+        bounded, steep_gap, near, far, ratio, power = [col(n) for n in ("bounded", "steep_gap", "near", "far", "ratio", "power")]
+        p = sb.tile([P, I], F32, name="p")
+        sums = col("sums", 2)
+        nc.scalar.activation(bounded[:], neg_max[:], ACT.Tanh, bias=th_unit[:], scale=1.0 / SPAN)
+        nc.gpsimd.tensor_scalar(steep_gap[:], neg_max[:], steep_c[:], steep_th[:], ALU.mult, ALU.add)
+        nc.scalar.activation(p[:], neg_a[:], ACT.Exp, bias=neg_max[:], scale=-1.0, accum_out=sums[:, 0:1])
+        nc.scalar.activation(near[:], bounded[:], ACT.Exp, scale=-SPAN)
+        nc.scalar.activation(far[:], bounded[:], ACT.Exp, bias=steep_gap[:], scale=neg_span_steep[:])
+        nc.scalar.activation(ratio[:], sums[:, 0:1], ACT.Copy, scale=near[:])
+        nc.gpsimd.tensor_tensor(power[:], ratio[:], neg_steep[:], ALU.pow)
+        nc.gpsimd.tensor_scalar(sums[:, 1:2], power[:], far[:], 1.0, ALU.mult, ALU.add)
+
+        v_picked = sb.tile([P, I], U16, name="v_picked", tag="picked_words", align_bytes=64)
+        v_scale = sb.tile([P, I], U8, name="v_scale", tag="picked_bytes", align_bytes=64)
+        nc.vector.tensor_copy(v_scale[:], v_bytes[:].indirect(offsets[:]))
+        old_hi = sb.tile([P, T // 2], F32, name="old_hi", tag="slot_b")
+        nc.sync.dma_start(old_hi[:], old[:, T // 2 : T])
+        c_bank = ps.tile([P, I], F32, name="c_bank")
+        for h in range(2):
+            nc.vector.tensor_copy(v_picked[:, halves[h]], v_words[:].indirect(half_offsets[h]))
+            product(c_bank[:, halves[h]], g_codes, g_plane, v_picked[:, halves[h]], v_scale[:, halves[h]])
+
+        inv, row_scale, slope, pull = col("inv", 2, tag="slot_c"), col("row_scale"), col("slope"), col("pull")
+        nc.vector.reciprocal(inv[:], sums[:])
+        nc.vector.tensor_scalar(row_scale[:], inv[:, 1:2], inv[:, 0:1], GRAD_SCALE, ALU.mult, ALU.mult)
+        nc.vector.tensor_scalar(slope[:], inv[:, 1:2], neg_steep[:], steep_less_one[:], ALU.mult, ALU.add)
+        nc.vector.tensor_scalar(pull[:], slope[:], inv[:, 0:1], row_scale[:], ALU.mult, ALU.mult)
+
+        own = sb.tile([P, I], F32, name="own")
+        own_sum = col("own_sum")
+        nc.vector.scalar_tensor_tensor(own[:], c_bank[:], kdot_c[:], p[:], ALU.subtract, ALU.mult, accum_out=own_sum[:])
+        own_scaled = sb.tile([P, I], F32, name="own_scaled")
+        shared = sb.tile([P, I], F32, name="shared")
+        nc.vector.tensor_scalar(own_scaled[:, halves[0]], own[:, halves[0]], row_scale[:], None, ALU.mult)
+        nc.scalar.activation(own_scaled[:, halves[1]], own[:, halves[1]], ACT.Copy, scale=row_scale[:])
+        nc.vector.tensor_scalar(shared[:], p[:], own_sum[:], pull[:], ALU.mult, ALU.mult)
+        nc.vector.tensor_tensor(placed[:].indirect(offsets[:]), own_scaled[:], shared[:], ALU.add)
+
+        start = 0
+        for n, width in enumerate(CHUNKS):
+            cols = slice(start, start + width)
+            before = old_lo[:, cols] if start < T // 2 else old_hi[:, start - T // 2 : start - T // 2 + width]
+            res = sb.tile([P, width], F32, name="res%d" % n)
+            nc.vector.tensor_tensor(res[:], placed[:, cols], before, ALU.add)
+            nc.sync.dma_start(out[:, cols], res[:])
+            start = start + width

@@ -21,7 +21,8 @@ PACK = 4
 HALF = I // 2
 GRAD_SCALE = 1024.0
 SPAN = 32.0
-CHUNKS = [128,384,512,512,512]
+OLD_SPLIT = 1280
+CHUNKS = [256,512,512,512,256]
 
 
 def tile_attend_bupdategate_s_kernel(tc, query, keys_words, keys_scales, th, steep, kdot, gout, vals_words, vals_scales, old, offs, out):
@@ -39,14 +40,13 @@ def tile_attend_bupdategate_s_kernel(tc, query, keys_words, keys_scales, th, ste
         k_words = sb.tile([P, T], U16, name="k_words")
         k_bytes = sb.tile([P, T], U8, name="k_bytes", tag="slot_a")
         v_bytes = sb.tile([P, T], U8, name="v_bytes", tag="slot_b")
-        q_raw = sb.tile([P, PACK, Q], F32, name="q_raw", tag="slot_c")
+        q_raw = sb.tile([P, PACK, Q], F32, name="q_raw")
+        v_words = sb.tile([P, T], U16, name="v_words", tag="slot_c")
         g_raw = sb.tile([P, PACK, Q], F32, name="g_raw")
         th_c, steep_c, kdot_c = col("th_c"), col("steep_c"), col("kdot_c")
         placed = sb.tile([P, T], F32, name="placed")
-        warm_in, warm_out = col("warm_in"), col("warm_out")
 
         nc.vector.memset(k_bytes[:].bitcast(I32), 0)
-        nc.vector.memset(warm_in[:], 0.0)
         nc.vector.memset(placed[:], 0.0)
         nc.vector.memset(v_bytes[:].bitcast(I32), 0)
 
@@ -58,9 +58,9 @@ def tile_attend_bupdategate_s_kernel(tc, query, keys_words, keys_scales, th, ste
         nc.sync.dma_start(k_words[:].bitcast(I32), keys_words[0].bitcast(I32))
         nc.sync.dma_start(q_raw[:], query.rearrange("(p j) w -> p j w", j=PACK))
         load_bytes(nc.scalar, k_bytes, keys_scales)
-        nc.scalar.activation(warm_out[:], warm_in[:], ACT.Exp)
-        nc.sync.dma_start(g_raw[:], gout.rearrange("(p j) w -> p j w", j=PACK))
+        nc.sync.dma_start(v_words[:].bitcast(I32), vals_words[0].bitcast(I32))
         nc.gpsimd.dma_start(th_c[:], th)
+        nc.gpsimd.dma_start(g_raw[:], gout.rearrange("(p j) w -> p j w", j=PACK))
         nc.gpsimd.dma_start(steep_c[:], steep)
         nc.gpsimd.dma_start(kdot_c[:], kdot)
         load_bytes(nc.sync, v_bytes, vals_scales)
@@ -81,68 +81,69 @@ def tile_attend_bupdategate_s_kernel(tc, query, keys_words, keys_scales, th, ste
         k_scale = sb.tile([P, I], U8, name="k_scale", tag="picked_bytes", align_bytes=64)
         nc.vector.tensor_copy(k_picked[:], k_words[:].indirect(offsets[:]))
         q_codes, q_plane = quantise(q_raw, "q")
-        v_words = sb.tile([P, T], U16, name="v_words", tag="slot_c")
-        nc.sync.dma_start(v_words[:].bitcast(I32), vals_words[0].bitcast(I32))
         g_codes, g_plane = quantise(g_raw, "g")
         a_banks = [ps.tile([P, HALF], F32, name="a_bank%d" % h) for h in range(2)]
         for h in range(2):
             nc.vector.tensor_copy(k_scale[:, halves[h]], k_bytes[:].indirect(half_offsets[h]))
             product(a_banks[h][:], q_codes, q_plane, k_picked[:, halves[h]], k_scale[:, halves[h]])
-        old_lo = sb.tile([P, T // 2], F32, name="old_lo", tag="slot_a")
-        nc.sync.dma_start(old_lo[:], old[:, 0 : T // 2])
+        old_lo = sb.tile([P, OLD_SPLIT], F32, name="old_lo", tag="slot_a")
+        nc.sync.dma_start(old_lo[:], old[:, 0:OLD_SPLIT])
         neg_a = sb.tile([P, I], F32, name="neg_a")
         neg_max_first, neg_max = col("neg_max_first"), col("neg_max")
         nc.vector.tensor_scalar(neg_a[:, halves[0]], a_banks[0][:], -1.0, None, ALU.mult, ALU.min, accum_out=neg_max_first[:])
         nc.vector.tensor_scalar(neg_a[:, halves[1]], a_banks[1][:], -1.0, neg_max_first[:], ALU.mult, ALU.min, accum_out=neg_max[:])
 
-        th_unit, steep_th, neg_steep, steep_less_one, neg_span_steep = [col(n) for n in ("th_unit", "steep_th", "neg_steep", "steep_less_one", "neg_span_steep")]
-        nc.gpsimd.tensor_scalar(th_unit[:], th_c[:], 1.0 / SPAN, 0.0, ALU.mult, ALU.add)
-        nc.gpsimd.tensor_scalar(steep_th[:], th_c[:], steep_c[:], 1.0, ALU.mult, ALU.mult)
-        nc.gpsimd.tensor_scalar(neg_span_steep[:], steep_c[:], -SPAN, 0.0, ALU.mult, ALU.add)
-        nc.gpsimd.tensor_scalar(neg_steep[:], steep_c[:], -1.0, 0.0, ALU.mult, ALU.add)
-        nc.gpsimd.tensor_scalar(steep_less_one[:], steep_c[:], 1.0, -1.0, ALU.mult, ALU.add)
-        bounded, steep_gap, near, far, ratio, power = [col(n) for n in ("bounded", "steep_gap", "near", "far", "ratio", "power")]
+        th_unit, neg_steep, steep_less_one, neg_steep_unit = [col(n) for n in ("th_unit", "neg_steep", "steep_less_one", "neg_steep_unit")]
+        nc.scalar.activation(th_unit[:], th_c[:], ACT.Copy, scale=1.0 / SPAN)
+        nc.scalar.activation(neg_steep[:], steep_c[:], ACT.Copy, scale=-1.0)
+        nc.scalar.activation(steep_less_one[:], steep_c[:], ACT.Copy, bias=-1.0)
+        nc.scalar.activation(neg_steep_unit[:], steep_c[:], ACT.Copy, scale=-1.0 / GRAD_SCALE)
+        bounded, gap, rest, near, far, ratio, power, z_unit, far_z = [col(n) for n in ("bounded", "gap", "rest", "near", "far", "ratio", "power", "z_unit", "far_z")]
         p = sb.tile([P, I], F32, name="p")
         sums = col("sums", 2)
         nc.scalar.activation(bounded[:], neg_max[:], ACT.Tanh, bias=th_unit[:], scale=1.0 / SPAN)
-        nc.gpsimd.tensor_scalar(steep_gap[:], neg_max[:], steep_c[:], steep_th[:], ALU.mult, ALU.add)
+        nc.scalar.activation(gap[:], neg_max[:], ACT.Identity, bias=th_c[:])
         nc.scalar.activation(p[:], neg_a[:], ACT.Exp, bias=neg_max[:], scale=-1.0, accum_out=sums[:, 0:1])
         nc.scalar.activation(near[:], bounded[:], ACT.Exp, scale=-SPAN)
-        nc.scalar.activation(far[:], bounded[:], ACT.Exp, bias=steep_gap[:], scale=neg_span_steep[:])
+        nc.scalar.activation(rest[:], bounded[:], ACT.Identity, bias=gap[:], scale=-SPAN)
         nc.scalar.activation(ratio[:], sums[:, 0:1], ACT.Copy, scale=near[:])
         nc.gpsimd.tensor_tensor(power[:], ratio[:], neg_steep[:], ALU.pow)
-        nc.gpsimd.tensor_scalar(sums[:, 1:2], power[:], far[:], 1.0, ALU.mult, ALU.add)
+        nc.scalar.activation(far[:], rest[:], ACT.Exp, scale=steep_c[:])
+        nc.scalar.activation(z_unit[:], sums[:, 0:1], ACT.Copy, scale=1.0 / GRAD_SCALE)
+        nc.scalar.activation(far_z[:], far[:], ACT.Copy, scale=z_unit[:])
+        nc.scalar.activation(sums[:, 1:2], power[:], ACT.Identity, bias=z_unit[:], scale=far_z[:])
 
         v_picked = sb.tile([P, I], U16, name="v_picked", tag="picked_words", align_bytes=64)
         v_scale = sb.tile([P, I], U8, name="v_scale", tag="picked_bytes", align_bytes=64)
-        nc.vector.tensor_copy(v_scale[:], v_bytes[:].indirect(offsets[:]))
-        old_hi = sb.tile([P, T // 2], F32, name="old_hi", tag="slot_b")
-        nc.sync.dma_start(old_hi[:], old[:, T // 2 : T])
+        nc.vector.tensor_copy(v_picked[:], v_words[:].indirect(offsets[:]))
+        old_hi = sb.tile([P, T - OLD_SPLIT], F32, name="old_hi", tag="slot_c")
+        nc.sync.dma_start(old_hi[:], old[:, OLD_SPLIT:T])
         c_bank = ps.tile([P, I], F32, name="c_bank")
         for h in range(2):
-            nc.vector.tensor_copy(v_picked[:, halves[h]], v_words[:].indirect(half_offsets[h]))
+            nc.vector.tensor_copy(v_scale[:, halves[h]], v_bytes[:].indirect(half_offsets[h]))
             product(c_bank[:, halves[h]], g_codes, g_plane, v_picked[:, halves[h]], v_scale[:, halves[h]])
 
-        inv, row_scale, slope, pull = col("inv", 2, tag="slot_c"), col("row_scale"), col("slope"), col("pull")
+        inv, base, slope, pull = col("inv", 2, tag="slot_b"), col("base"), col("slope"), col("pull")
         nc.vector.reciprocal(inv[:], sums[:])
-        nc.vector.tensor_scalar(row_scale[:], inv[:, 1:2], inv[:, 0:1], GRAD_SCALE, ALU.mult, ALU.mult)
-        nc.vector.tensor_scalar(slope[:], inv[:, 1:2], neg_steep[:], steep_less_one[:], ALU.mult, ALU.add)
-        nc.vector.tensor_scalar(pull[:], slope[:], inv[:, 0:1], row_scale[:], ALU.mult, ALU.mult)
+        row_scale = inv[:, 1:2]
+        nc.scalar.activation(base[:], inv[:, 0:1], ACT.Copy, scale=steep_less_one[:])
+        nc.scalar.activation(slope[:], row_scale, ACT.Identity, bias=base[:], scale=neg_steep_unit[:])
+        nc.scalar.activation(pull[:], slope[:], ACT.Copy, scale=row_scale)
 
         own = sb.tile([P, I], F32, name="own")
         own_sum = col("own_sum")
         nc.vector.scalar_tensor_tensor(own[:], c_bank[:], kdot_c[:], p[:], ALU.subtract, ALU.mult, accum_out=own_sum[:])
         own_scaled = sb.tile([P, I], F32, name="own_scaled")
         shared = sb.tile([P, I], F32, name="shared")
-        nc.vector.tensor_scalar(own_scaled[:, halves[0]], own[:, halves[0]], row_scale[:], None, ALU.mult)
-        nc.scalar.activation(own_scaled[:, halves[1]], own[:, halves[1]], ACT.Copy, scale=row_scale[:])
+        nc.vector.tensor_scalar(own_scaled[:, halves[0]], own[:, halves[0]], row_scale, None, ALU.mult)
+        nc.scalar.activation(own_scaled[:, halves[1]], own[:, halves[1]], ACT.Copy, scale=row_scale)
         nc.vector.tensor_scalar(shared[:], p[:], own_sum[:], pull[:], ALU.mult, ALU.mult)
         nc.vector.tensor_tensor(placed[:].indirect(offsets[:]), own_scaled[:], shared[:], ALU.add)
 
         start = 0
         for n, width in enumerate(CHUNKS):
             cols = slice(start, start + width)
-            before = old_lo[:, cols] if start < T // 2 else old_hi[:, start - T // 2 : start - T // 2 + width]
+            before = old_lo[:, cols] if start < OLD_SPLIT else old_hi[:, start - OLD_SPLIT : start - OLD_SPLIT + width]
             res = sb.tile([P, width], F32, name="res%d" % n)
             nc.vector.tensor_tensor(res[:], placed[:, cols], before, ALU.add)
             nc.sync.dma_start(out[:, cols], res[:])

@@ -21,7 +21,6 @@ PACK = 4
 HALF = I // 2
 GRAD_SCALE = 1024.0
 SPAN = 32.0
-OLD_SPLIT = 1280
 CHUNKS = [256,512,512,512,256]
 
 
@@ -38,17 +37,18 @@ def tile_attend_bupdategate_s_kernel(tc, query, keys_words, keys_scales, th, ste
         halves = [slice(h * HALF, (h + 1) * HALF) for h in range(2)]
         half_offsets = [offsets[:, h * (HALF // 16) : (h + 1) * (HALF // 16)] for h in range(2)]
         k_words = sb.tile([P, T], U16, name="k_words")
-        k_bytes = sb.tile([P, T], U8, name="k_bytes", tag="slot_a")
+        k_bytes = sb.tile([P, T], U8, name="k_bytes")
         v_bytes = sb.tile([P, T], U8, name="v_bytes", tag="slot_b")
         q_raw = sb.tile([P, PACK, Q], F32, name="q_raw")
-        v_words = sb.tile([P, T], U16, name="v_words", tag="slot_c")
+        v_words = sb.tile([P, T], U16, name="v_words")
         g_raw = sb.tile([P, PACK, Q], F32, name="g_raw")
         th_c, steep_c, kdot_c = col("th_c"), col("steep_c"), col("kdot_c")
         placed = sb.tile([P, T], F32, name="placed")
+        old_sb = sb.tile([P, T], F32, name="old_sb")
 
         nc.vector.memset(k_bytes[:].bitcast(I32), 0)
-        nc.vector.memset(placed[:], 0.0)
         nc.vector.memset(v_bytes[:].bitcast(I32), 0)
+        nc.vector.memset(placed[:].bitcast(I32), 0)
 
         def load_bytes(queue, tile, scales):
             for quad in range(4):
@@ -57,13 +57,14 @@ def tile_attend_bupdategate_s_kernel(tc, query, keys_words, keys_scales, th, ste
         nc.sync.dma_start(offsets[:], offs)
         nc.sync.dma_start(k_words[:].bitcast(I32), keys_words[0].bitcast(I32))
         nc.sync.dma_start(q_raw[:], query.rearrange("(p j) w -> p j w", j=PACK))
-        load_bytes(nc.scalar, k_bytes, keys_scales)
+        load_bytes(nc.sync, k_bytes, keys_scales)
+        nc.sync.dma_start(g_raw[:], gout.rearrange("(p j) w -> p j w", j=PACK))
         nc.sync.dma_start(v_words[:].bitcast(I32), vals_words[0].bitcast(I32))
-        nc.gpsimd.dma_start(th_c[:], th)
-        nc.gpsimd.dma_start(g_raw[:], gout.rearrange("(p j) w -> p j w", j=PACK))
-        nc.gpsimd.dma_start(steep_c[:], steep)
-        nc.gpsimd.dma_start(kdot_c[:], kdot)
+        nc.sync.dma_start(th_c[:], th)
+        nc.sync.dma_start(steep_c[:], steep)
         load_bytes(nc.sync, v_bytes, vals_scales)
+        nc.sync.dma_start(kdot_c[:], kdot)
+        nc.sync.dma_start(old_sb[:], old)
 
         def quantise(raw, name):
             woven = sb.tile([P, Q, PACK], BF16, name=name + "_woven", align_bytes=64)
@@ -86,8 +87,6 @@ def tile_attend_bupdategate_s_kernel(tc, query, keys_words, keys_scales, th, ste
         for h in range(2):
             nc.vector.tensor_copy(k_scale[:, halves[h]], k_bytes[:].indirect(half_offsets[h]))
             product(a_banks[h][:], q_codes, q_plane, k_picked[:, halves[h]], k_scale[:, halves[h]])
-        old_lo = sb.tile([P, OLD_SPLIT], F32, name="old_lo", tag="slot_a")
-        nc.sync.dma_start(old_lo[:], old[:, 0:OLD_SPLIT])
         neg_a = sb.tile([P, I], F32, name="neg_a")
         neg_max_first, neg_max = col("neg_max_first"), col("neg_max")
         nc.vector.tensor_scalar(neg_a[:, halves[0]], a_banks[0][:], -1.0, None, ALU.mult, ALU.min, accum_out=neg_max_first[:])
@@ -116,8 +115,6 @@ def tile_attend_bupdategate_s_kernel(tc, query, keys_words, keys_scales, th, ste
         v_picked = sb.tile([P, I], U16, name="v_picked", tag="picked_words", align_bytes=64)
         v_scale = sb.tile([P, I], U8, name="v_scale", tag="picked_bytes", align_bytes=64)
         nc.vector.tensor_copy(v_picked[:], v_words[:].indirect(offsets[:]))
-        old_hi = sb.tile([P, T - OLD_SPLIT], F32, name="old_hi", tag="slot_c")
-        nc.sync.dma_start(old_hi[:], old[:, OLD_SPLIT:T])
         c_bank = ps.tile([P, I], F32, name="c_bank")
         for h in range(2):
             nc.vector.tensor_copy(v_scale[:, halves[h]], v_bytes[:].indirect(half_offsets[h]))
@@ -143,8 +140,7 @@ def tile_attend_bupdategate_s_kernel(tc, query, keys_words, keys_scales, th, ste
         start = 0
         for n, width in enumerate(CHUNKS):
             cols = slice(start, start + width)
-            before = old_lo[:, cols] if start < OLD_SPLIT else old_hi[:, start - OLD_SPLIT : start - OLD_SPLIT + width]
             res = sb.tile([P, width], F32, name="res%d" % n)
-            nc.vector.tensor_tensor(res[:], placed[:, cols], before, ALU.add)
+            nc.vector.tensor_tensor(res[:], placed[:, cols], old_sb[:, cols], ALU.add)
             nc.sync.dma_start(out[:, cols], res[:])
             start = start + width

@@ -59,8 +59,8 @@ def tile_attend_bupdategate_s_kernel(tc, query, keys_words, keys_scales, th, ste
         nc.sync.dma_start(q_raw[:], query.rearrange("(p j) w -> p j w", j=PACK))
         load_bytes(nc.sync, k_bytes, keys_scales)
         nc.sync.dma_start(g_raw[:], gout.rearrange("(p j) w -> p j w", j=PACK))
-        nc.sync.dma_start(v_words[:].bitcast(I32), vals_words[0].bitcast(I32))
         nc.sync.dma_start(th_c[:], th)
+        nc.sync.dma_start(v_words[:].bitcast(I32), vals_words[0].bitcast(I32))
         nc.sync.dma_start(steep_c[:], steep)
         load_bytes(nc.sync, v_bytes, vals_scales)
         nc.sync.dma_start(kdot_c[:], kdot)
@@ -70,7 +70,7 @@ def tile_attend_bupdategate_s_kernel(tc, query, keys_words, keys_scales, th, ste
             woven = sb.tile([P, Q, PACK], BF16, name=name + "_woven", align_bytes=64)
             codes = sb.tile([P, Q], U32, name=name + "_codes", align_bytes=64)
             plane = sb.tile([P, Q], U8, name=name + "_plane", align_bytes=64)
-            nc.scalar.copy(woven[:], raw[:].rearrange("p j w -> p w j"))
+            nc.scalar.copy(woven[:].rearrange("p (c i) j -> p c j i", i=4), raw[:].rearrange("p j (c i) -> p c j i", i=4))
             nc.vector.quantize_mx(out=codes[:].bitcast(FP8X4), scales=plane[:], in_=woven[:].rearrange("p w j -> p (w j)"))
             return codes, plane
 
@@ -87,16 +87,13 @@ def tile_attend_bupdategate_s_kernel(tc, query, keys_words, keys_scales, th, ste
         for h in range(2):
             nc.vector.tensor_copy(k_scale[:, halves[h]], k_bytes[:].indirect(half_offsets[h]))
             product(a_banks[h][:], q_codes, q_plane, k_picked[:, halves[h]], k_scale[:, halves[h]])
-        neg_a = sb.tile([P, I], F32, name="neg_a")
+        neg_a = sb.tile([P, I], F32, name="neg_a", tag="slot_a")
         neg_max_first, neg_max = col("neg_max_first"), col("neg_max")
         nc.vector.tensor_scalar(neg_a[:, halves[0]], a_banks[0][:], -1.0, None, ALU.mult, ALU.min, accum_out=neg_max_first[:])
         nc.vector.tensor_scalar(neg_a[:, halves[1]], a_banks[1][:], -1.0, neg_max_first[:], ALU.mult, ALU.min, accum_out=neg_max[:])
 
-        th_unit, neg_steep, steep_less_one, neg_steep_unit = [col(n) for n in ("th_unit", "neg_steep", "steep_less_one", "neg_steep_unit")]
+        th_unit = col("th_unit")
         nc.scalar.activation(th_unit[:], th_c[:], ACT.Copy, scale=1.0 / SPAN)
-        nc.scalar.activation(neg_steep[:], steep_c[:], ACT.Copy, scale=-1.0)
-        nc.scalar.activation(steep_less_one[:], steep_c[:], ACT.Copy, bias=-1.0)
-        nc.scalar.activation(neg_steep_unit[:], steep_c[:], ACT.Copy, scale=-1.0 / GRAD_SCALE)
         bounded, gap, rest, near, far, ratio, power, z_unit, far_z = [col(n) for n in ("bounded", "gap", "rest", "near", "far", "ratio", "power", "z_unit", "far_z")]
         p = sb.tile([P, I], F32, name="p")
         sums = col("sums", 2)
@@ -104,37 +101,42 @@ def tile_attend_bupdategate_s_kernel(tc, query, keys_words, keys_scales, th, ste
         nc.scalar.activation(gap[:], neg_max[:], ACT.Identity, bias=th_c[:])
         nc.scalar.activation(p[:], neg_a[:], ACT.Exp, bias=neg_max[:], scale=-1.0, accum_out=sums[:, 0:1])
         nc.scalar.activation(near[:], bounded[:], ACT.Exp, scale=-SPAN)
-        nc.scalar.activation(rest[:], bounded[:], ACT.Identity, bias=gap[:], scale=-SPAN)
+        derived = col("derived", 3, tag="slot_a")
+        neg_steep, steep_less_one, neg_steep_unit = [derived[:, n : n + 1] for n in range(3)]
+        nc.scalar.activation(neg_steep, steep_c[:], ACT.Copy, scale=-1.0)
         nc.scalar.activation(ratio[:], sums[:, 0:1], ACT.Copy, scale=near[:])
-        nc.gpsimd.tensor_tensor(power[:], ratio[:], neg_steep[:], ALU.pow)
+        nc.gpsimd.tensor_tensor(power[:], ratio[:], neg_steep, ALU.pow)
+        nc.scalar.activation(rest[:], bounded[:], ACT.Identity, bias=gap[:], scale=-SPAN)
         nc.scalar.activation(far[:], rest[:], ACT.Exp, scale=steep_c[:])
         nc.scalar.activation(z_unit[:], sums[:, 0:1], ACT.Copy, scale=1.0 / GRAD_SCALE)
         nc.scalar.activation(far_z[:], far[:], ACT.Copy, scale=z_unit[:])
+        nc.scalar.activation(steep_less_one, steep_c[:], ACT.Copy, bias=-1.0)
+        nc.scalar.activation(neg_steep_unit, steep_c[:], ACT.Copy, scale=-1.0 / GRAD_SCALE)
         nc.scalar.activation(sums[:, 1:2], power[:], ACT.Identity, bias=z_unit[:], scale=far_z[:])
 
         v_picked = sb.tile([P, I], U16, name="v_picked", tag="picked_words", align_bytes=64)
         v_scale = sb.tile([P, I], U8, name="v_scale", tag="picked_bytes", align_bytes=64)
         nc.vector.tensor_copy(v_picked[:], v_words[:].indirect(offsets[:]))
-        c_bank = ps.tile([P, I], F32, name="c_bank")
+        c_banks = [ps.tile([P, HALF], F32, name="c_bank%d" % h) for h in range(2)]
         for h in range(2):
             nc.vector.tensor_copy(v_scale[:, halves[h]], v_bytes[:].indirect(half_offsets[h]))
-            product(c_bank[:, halves[h]], g_codes, g_plane, v_picked[:, halves[h]], v_scale[:, halves[h]])
+            product(c_banks[h][:], g_codes, g_plane, v_picked[:, halves[h]], v_scale[:, halves[h]])
 
         inv, base, slope, pull = col("inv", 2, tag="slot_b"), col("base"), col("slope"), col("pull")
         nc.vector.reciprocal(inv[:], sums[:])
         row_scale = inv[:, 1:2]
-        nc.scalar.activation(base[:], inv[:, 0:1], ACT.Copy, scale=steep_less_one[:])
-        nc.scalar.activation(slope[:], row_scale, ACT.Identity, bias=base[:], scale=neg_steep_unit[:])
-        nc.scalar.activation(pull[:], slope[:], ACT.Copy, scale=row_scale)
+        nc.scalar.activation(base[:], inv[:, 0:1], ACT.Copy, scale=steep_less_one)
+        nc.scalar.activation(slope[:], row_scale, ACT.Identity, bias=base[:], scale=neg_steep_unit)
 
         own = sb.tile([P, I], F32, name="own")
-        own_sum = col("own_sum")
-        nc.vector.scalar_tensor_tensor(own[:], c_bank[:], kdot_c[:], p[:], ALU.subtract, ALU.mult, accum_out=own_sum[:])
+        own_sums = col("own_sums", 2)
         own_scaled = sb.tile([P, I], F32, name="own_scaled")
         shared = sb.tile([P, I], F32, name="shared")
-        nc.vector.tensor_scalar(own_scaled[:, halves[0]], own[:, halves[0]], row_scale, None, ALU.mult)
-        nc.scalar.activation(own_scaled[:, halves[1]], own[:, halves[1]], ACT.Copy, scale=row_scale)
-        nc.vector.tensor_scalar(shared[:], p[:], own_sum[:], pull[:], ALU.mult, ALU.mult)
+        for h in range(2):
+            nc.vector.scalar_tensor_tensor(own[:, halves[h]], c_banks[h][:], kdot_c[:], p[:, halves[h]], ALU.subtract, ALU.mult, accum_out=own_sums[:, h : h + 1])
+            nc.scalar.activation(own_scaled[:, halves[h]], own[:, halves[h]], ACT.Copy, scale=row_scale)
+        nc.vector.tensor_scalar(pull[:], own_sums[:, 0:1], own_sums[:, 1:2], slope[:], ALU.add, ALU.mult)
+        nc.vector.tensor_scalar(shared[:], p[:], pull[:], row_scale, ALU.mult, ALU.mult)
         nc.vector.tensor_tensor(placed[:].indirect(offsets[:]), own_scaled[:], shared[:], ALU.add)
 
         start = 0

@@ -18,10 +18,13 @@ ACT = mybir.ActivationFunctionType
 
 P = 128
 PACK = 4
+QUADRANTS, QUADRANT_ROWS, SCALE_ROWS = 4, 32, 4
+LANES = 16
+LINE = 4
 HALF = I // 2
 GRAD_SCALE = 1024.0
 SPAN = 32.0
-CHUNKS = [256,512,512,512,256]
+CHUNKS = (128, 384, 512, 512, 384, 128)
 
 
 def tile_attend_bupdategate_s_kernel(tc, query, keys_words, keys_scales, th, steep, kdot, gout, vals_words, vals_scales, old, offs, out):
@@ -33,12 +36,12 @@ def tile_attend_bupdategate_s_kernel(tc, query, keys_words, keys_scales, th, ste
         def col(name, width=1, tag=""):
             return sb.tile([P, width], F32, name=name, tag=tag)
 
-        offsets = sb.tile([P, I // 16], U16, name="offsets")
+        offsets = sb.tile([P, I // LANES], U16, name="offsets")
         halves = [slice(h * HALF, (h + 1) * HALF) for h in range(2)]
-        half_offsets = [offsets[:, h * (HALF // 16) : (h + 1) * (HALF // 16)] for h in range(2)]
+        half_offsets = [offsets[:, h * (HALF // LANES) : (h + 1) * (HALF // LANES)] for h in range(2)]
         k_words = sb.tile([P, T], U16, name="k_words")
         k_bytes = sb.tile([P, T], U8, name="k_bytes")
-        v_bytes = sb.tile([P, T], U8, name="v_bytes", tag="slot_b")
+        v_bytes = sb.tile([P, T], U8, name="v_bytes", tag="v_bytes_then_inv")
         q_raw = sb.tile([P, PACK, Q], F32, name="q_raw")
         v_words = sb.tile([P, T], U16, name="v_words")
         g_raw = sb.tile([P, PACK, Q], F32, name="g_raw")
@@ -50,69 +53,74 @@ def tile_attend_bupdategate_s_kernel(tc, query, keys_words, keys_scales, th, ste
         nc.vector.memset(v_bytes[:].bitcast(I32), 0)
         nc.vector.memset(placed[:].bitcast(I32), 0)
 
-        def load_bytes(queue, tile, scales):
-            for quad in range(4):
-                queue.dma_start(tile[32 * quad : 32 * quad + 4, :].bitcast(I32), scales[0, 4 * quad : 4 * quad + 4, :].bitcast(I32))
+        def load_scale_bytes(tile, scales):
+            for quad in range(QUADRANTS):
+                rows = slice(QUADRANT_ROWS * quad, QUADRANT_ROWS * quad + SCALE_ROWS)
+                nc.sync.dma_start(tile[rows, :].bitcast(I32), scales[0, SCALE_ROWS * quad : SCALE_ROWS * (quad + 1), :].bitcast(I32))
 
-        nc.sync.dma_start(offsets[:], offs)
         nc.sync.dma_start(k_words[:].bitcast(I32), keys_words[0].bitcast(I32))
+        nc.sync.dma_start(offsets[:], offs)
         nc.sync.dma_start(q_raw[:], query.rearrange("(p j) w -> p j w", j=PACK))
-        load_bytes(nc.sync, k_bytes, keys_scales)
+        load_scale_bytes(k_bytes, keys_scales)
         nc.sync.dma_start(g_raw[:], gout.rearrange("(p j) w -> p j w", j=PACK))
         nc.sync.dma_start(th_c[:], th)
         nc.sync.dma_start(v_words[:].bitcast(I32), vals_words[0].bitcast(I32))
         nc.sync.dma_start(steep_c[:], steep)
-        load_bytes(nc.sync, v_bytes, vals_scales)
+        load_scale_bytes(v_bytes, vals_scales)
         nc.sync.dma_start(kdot_c[:], kdot)
         nc.sync.dma_start(old_sb[:], old)
 
         def quantise(raw, name):
             woven = sb.tile([P, Q, PACK], BF16, name=name + "_woven", align_bytes=64)
             codes = sb.tile([P, Q], U32, name=name + "_codes", align_bytes=64)
-            plane = sb.tile([P, Q], U8, name=name + "_plane", align_bytes=64)
-            nc.scalar.copy(woven[:].rearrange("p (c i) j -> p c j i", i=4), raw[:].rearrange("p j (c i) -> p c j i", i=4))
-            nc.vector.quantize_mx(out=codes[:].bitcast(FP8X4), scales=plane[:], in_=woven[:].rearrange("p w j -> p (w j)"))
-            return codes, plane
+            block_scales = sb.tile([P, Q], U8, name=name + "_block_scales", align_bytes=64)
+            nc.scalar.copy(woven[:].rearrange("p (c i) j -> p c j i", i=LINE), raw[:].rearrange("p j (c i) -> p c j i", i=LINE))
+            nc.vector.quantize_mx(out=codes[:].bitcast(FP8X4), scales=block_scales[:], in_=woven[:].rearrange("p w j -> p (w j)"))
+            return codes, block_scales
 
-        def product(bank, codes, plane, words, scale_bytes):
-            nc.tensor.matmul_mx(out=bank, lhsT=codes[:].bitcast(FP8X4), lhsT_scale=plane[:],
-                                rhs=words.bitcast(FP4X4), rhs_scale=scale_bytes, start=True, stop=True)
+        def product(bank, codes, block_scales, picked_words, picked_bytes):
+            nc.tensor.matmul_mx(out=bank, lhsT=codes[:].bitcast(FP8X4), lhsT_scale=block_scales[:],
+                                rhs=picked_words.bitcast(FP4X4), rhs_scale=picked_bytes, start=True, stop=True)
 
         k_picked = sb.tile([P, I], U16, name="k_picked", tag="picked_words", align_bytes=64)
         k_scale = sb.tile([P, I], U8, name="k_scale", tag="picked_bytes", align_bytes=64)
         nc.vector.tensor_copy(k_picked[:], k_words[:].indirect(offsets[:]))
-        q_codes, q_plane = quantise(q_raw, "q")
-        g_codes, g_plane = quantise(g_raw, "g")
+        q_codes, q_block_scales = quantise(q_raw, "q")
+        g_codes, g_block_scales = quantise(g_raw, "g")
         a_banks = [ps.tile([P, HALF], F32, name="a_bank%d" % h) for h in range(2)]
         for h in range(2):
             nc.vector.tensor_copy(k_scale[:, halves[h]], k_bytes[:].indirect(half_offsets[h]))
-            product(a_banks[h][:], q_codes, q_plane, k_picked[:, halves[h]], k_scale[:, halves[h]])
-        neg_a = sb.tile([P, I], F32, name="neg_a", tag="slot_a")
+            product(a_banks[h][:], q_codes, q_block_scales, k_picked[:, halves[h]], k_scale[:, halves[h]])
+
+        neg_a = sb.tile([P, I], F32, name="neg_a", tag="neg_a_then_steep_forms")
         neg_max_first, neg_max = col("neg_max_first"), col("neg_max")
         nc.vector.tensor_scalar(neg_a[:, halves[0]], a_banks[0][:], -1.0, None, ALU.mult, ALU.min, accum_out=neg_max_first[:])
         nc.vector.tensor_scalar(neg_a[:, halves[1]], a_banks[1][:], -1.0, neg_max_first[:], ALU.mult, ALU.min, accum_out=neg_max[:])
 
         th_unit = col("th_unit")
         nc.scalar.activation(th_unit[:], th_c[:], ACT.Copy, scale=1.0 / SPAN)
-        bounded, gap, rest, near, far, ratio, power, z_unit, far_z = [col(n) for n in ("bounded", "gap", "rest", "near", "far", "ratio", "power", "z_unit", "far_z")]
+        bounded, gap, rest, near, far, ratio, power, z_unit, far_z = [
+            col(name) for name in ("bounded", "gap", "rest", "near", "far", "ratio", "power", "z_unit", "far_z")
+        ]
         p = sb.tile([P, I], F32, name="p")
-        sums = col("sums", 2)
+        denominators = col("denominators", 2)
+        z = denominators[:, 0:1]
         nc.scalar.activation(bounded[:], neg_max[:], ACT.Tanh, bias=th_unit[:], scale=1.0 / SPAN)
         nc.scalar.activation(gap[:], neg_max[:], ACT.Identity, bias=th_c[:])
-        nc.scalar.activation(p[:], neg_a[:], ACT.Exp, bias=neg_max[:], scale=-1.0, accum_out=sums[:, 0:1])
+        nc.scalar.activation(p[:], neg_a[:], ACT.Exp, bias=neg_max[:], scale=-1.0, accum_out=z)
         nc.scalar.activation(near[:], bounded[:], ACT.Exp, scale=-SPAN)
-        derived = col("derived", 3, tag="slot_a")
-        neg_steep, steep_less_one, neg_steep_unit = [derived[:, n : n + 1] for n in range(3)]
+        steep_forms = col("steep_forms", 3, tag="neg_a_then_steep_forms")
+        neg_steep, steep_less_one, neg_steep_unit = [steep_forms[:, n : n + 1] for n in range(3)]
         nc.scalar.activation(neg_steep, steep_c[:], ACT.Copy, scale=-1.0)
-        nc.scalar.activation(ratio[:], sums[:, 0:1], ACT.Copy, scale=near[:])
+        nc.scalar.activation(ratio[:], z, ACT.Copy, scale=near[:])
         nc.gpsimd.tensor_tensor(power[:], ratio[:], neg_steep, ALU.pow)
         nc.scalar.activation(rest[:], bounded[:], ACT.Identity, bias=gap[:], scale=-SPAN)
         nc.scalar.activation(far[:], rest[:], ACT.Exp, scale=steep_c[:])
-        nc.scalar.activation(z_unit[:], sums[:, 0:1], ACT.Copy, scale=1.0 / GRAD_SCALE)
+        nc.scalar.activation(z_unit[:], z, ACT.Copy, scale=1.0 / GRAD_SCALE)
         nc.scalar.activation(far_z[:], far[:], ACT.Copy, scale=z_unit[:])
         nc.scalar.activation(steep_less_one, steep_c[:], ACT.Copy, bias=-1.0)
         nc.scalar.activation(neg_steep_unit, steep_c[:], ACT.Copy, scale=-1.0 / GRAD_SCALE)
-        nc.scalar.activation(sums[:, 1:2], power[:], ACT.Identity, bias=z_unit[:], scale=far_z[:])
+        nc.scalar.activation(denominators[:, 1:2], power[:], ACT.Identity, bias=z_unit[:], scale=far_z[:])
 
         v_picked = sb.tile([P, I], U16, name="v_picked", tag="picked_words", align_bytes=64)
         v_scale = sb.tile([P, I], U8, name="v_scale", tag="picked_bytes", align_bytes=64)
@@ -120,12 +128,12 @@ def tile_attend_bupdategate_s_kernel(tc, query, keys_words, keys_scales, th, ste
         c_banks = [ps.tile([P, HALF], F32, name="c_bank%d" % h) for h in range(2)]
         for h in range(2):
             nc.vector.tensor_copy(v_scale[:, halves[h]], v_bytes[:].indirect(half_offsets[h]))
-            product(c_banks[h][:], g_codes, g_plane, v_picked[:, halves[h]], v_scale[:, halves[h]])
+            product(c_banks[h][:], g_codes, g_block_scales, v_picked[:, halves[h]], v_scale[:, halves[h]])
 
-        inv, base, slope, pull = col("inv", 2, tag="slot_b"), col("base"), col("slope"), col("pull")
-        nc.vector.reciprocal(inv[:], sums[:])
-        row_scale = inv[:, 1:2]
-        nc.scalar.activation(base[:], inv[:, 0:1], ACT.Copy, scale=steep_less_one)
+        inv, base, slope, pull = col("inv", 2, tag="v_bytes_then_inv"), col("base"), col("slope"), col("pull")
+        nc.vector.reciprocal(inv[:], denominators[:])
+        inv_z, row_scale = inv[:, 0:1], inv[:, 1:2]
+        nc.scalar.activation(base[:], inv_z, ACT.Copy, scale=steep_less_one)
         nc.scalar.activation(slope[:], row_scale, ACT.Identity, bias=base[:], scale=neg_steep_unit)
 
         own = sb.tile([P, I], F32, name="own")
@@ -142,7 +150,7 @@ def tile_attend_bupdategate_s_kernel(tc, query, keys_words, keys_scales, th, ste
         start = 0
         for n, width in enumerate(CHUNKS):
             cols = slice(start, start + width)
-            res = sb.tile([P, width], F32, name="res%d" % n)
-            nc.vector.tensor_tensor(res[:], placed[:, cols], old_sb[:, cols], ALU.add)
-            nc.sync.dma_start(out[:, cols], res[:])
+            total = sb.tile([P, width], F32, name="total%d" % n)
+            nc.vector.tensor_tensor(total[:], placed[:, cols], old_sb[:, cols], ALU.add)
+            nc.sync.dma_start(out[:, cols], total[:])
             start = start + width

from contextlib import ExitStack

import concourse.mybir as mybir

D, T, I, Q = 512, 2048, 512, 128
FLOPS = 2 * 2 * D * I * Q

F32 = mybir.dt.float32
BF16 = mybir.dt.bfloat16
I32 = mybir.dt.int32
U32 = mybir.dt.uint32
U16 = mybir.dt.uint16
U8 = mybir.dt.uint8
FP8X4 = mybir.dt.float8_e4m3fn_x4
FP4X4 = mybir.dt.float4_e2m1fn_x4
ALU = mybir.AluOpType
ACT = mybir.ActivationFunctionType

P = 128
PACK = 4
QUADRANTS, QUADRANT_ROWS, SCALE_ROWS = 4, 32, 4
LANES = 16
LINE = 4
HALF = I // 2
GRAD_SCALE = 1024.0
SPAN = 32.0
CHUNKS = (128, 384, 512, 512, 384, 128)


def tile_attend_bupdategate_s_kernel(tc, query, keys_words, keys_scales, th, steep, kdot, gout, vals_words, vals_scales, old, offs, out):
    nc = tc.nc
    with ExitStack() as ctx:
        sb = ctx.enter_context(tc.tile_pool(name="sb", bufs=1))
        ps = ctx.enter_context(tc.psum_pool(name="ps", bufs=1))

        def col(name, width=1, tag=""):
            return sb.tile([P, width], F32, name=name, tag=tag)

        offsets = sb.tile([P, I // LANES], U16, name="offsets")
        halves = [slice(h * HALF, (h + 1) * HALF) for h in range(2)]
        half_offsets = [offsets[:, h * (HALF // LANES) : (h + 1) * (HALF // LANES)] for h in range(2)]
        k_words = sb.tile([P, T], U16, name="k_words")
        k_bytes = sb.tile([P, T], U8, name="k_bytes")
        v_bytes = sb.tile([P, T], U8, name="v_bytes", tag="v_bytes_then_inv")
        q_raw = sb.tile([P, PACK, Q], F32, name="q_raw")
        v_words = sb.tile([P, T], U16, name="v_words")
        g_raw = sb.tile([P, PACK, Q], F32, name="g_raw")
        th_c, steep_c, kdot_c = col("th_c"), col("steep_c"), col("kdot_c")
        placed = sb.tile([P, T], F32, name="placed")
        old_sb = sb.tile([P, T], F32, name="old_sb")

        nc.vector.memset(k_bytes[:].bitcast(I32), 0)
        nc.vector.memset(v_bytes[:].bitcast(I32), 0)
        nc.vector.memset(placed[:].bitcast(I32), 0)

        def load_scale_bytes(tile, scales):
            for quad in range(QUADRANTS):
                rows = slice(QUADRANT_ROWS * quad, QUADRANT_ROWS * quad + SCALE_ROWS)
                nc.sync.dma_start(tile[rows, :].bitcast(I32), scales[0, SCALE_ROWS * quad : SCALE_ROWS * (quad + 1), :].bitcast(I32))

        nc.sync.dma_start(k_words[:].bitcast(I32), keys_words[0].bitcast(I32))
        nc.sync.dma_start(offsets[:], offs)
        nc.sync.dma_start(q_raw[:], query.rearrange("(p j) w -> p j w", j=PACK))
        load_scale_bytes(k_bytes, keys_scales)
        nc.sync.dma_start(g_raw[:], gout.rearrange("(p j) w -> p j w", j=PACK))
        nc.sync.dma_start(th_c[:], th)
        nc.sync.dma_start(v_words[:].bitcast(I32), vals_words[0].bitcast(I32))
        nc.sync.dma_start(steep_c[:], steep)
        load_scale_bytes(v_bytes, vals_scales)
        nc.sync.dma_start(kdot_c[:], kdot)
        nc.sync.dma_start(old_sb[:], old)

        def quantise(raw, name):
            woven = sb.tile([P, Q, PACK], BF16, name=name + "_woven", align_bytes=64)
            codes = sb.tile([P, Q], U32, name=name + "_codes", align_bytes=64)
            block_scales = sb.tile([P, Q], U8, name=name + "_block_scales", align_bytes=64)
            nc.scalar.copy(woven[:].rearrange("p (c i) j -> p c j i", i=LINE), raw[:].rearrange("p j (c i) -> p c j i", i=LINE))
            nc.vector.quantize_mx(out=codes[:].bitcast(FP8X4), scales=block_scales[:], in_=woven[:].rearrange("p w j -> p (w j)"))
            return codes, block_scales

        def product(bank, codes, block_scales, picked_words, picked_bytes):
            nc.tensor.matmul_mx(out=bank, lhsT=codes[:].bitcast(FP8X4), lhsT_scale=block_scales[:],
                                rhs=picked_words.bitcast(FP4X4), rhs_scale=picked_bytes, start=True, stop=True)

        k_picked = sb.tile([P, I], U16, name="k_picked", tag="picked_words", align_bytes=64)
        k_scale = sb.tile([P, I], U8, name="k_scale", tag="picked_bytes", align_bytes=64)
        nc.vector.tensor_copy(k_picked[:], k_words[:].indirect(offsets[:]))
        q_codes, q_block_scales = quantise(q_raw, "q")
        g_codes, g_block_scales = quantise(g_raw, "g")
        a_banks = [ps.tile([P, HALF], F32, name="a_bank%d" % h) for h in range(2)]
        for h in range(2):
            nc.vector.tensor_copy(k_scale[:, halves[h]], k_bytes[:].indirect(half_offsets[h]))
            product(a_banks[h][:], q_codes, q_block_scales, k_picked[:, halves[h]], k_scale[:, halves[h]])

        neg_a = sb.tile([P, I], F32, name="neg_a", tag="neg_a_then_steep_forms")
        neg_max_first, neg_max = col("neg_max_first"), col("neg_max")
        nc.vector.tensor_scalar(neg_a[:, halves[0]], a_banks[0][:], -1.0, None, ALU.mult, ALU.min, accum_out=neg_max_first[:])
        nc.vector.tensor_scalar(neg_a[:, halves[1]], a_banks[1][:], -1.0, neg_max_first[:], ALU.mult, ALU.min, accum_out=neg_max[:])

        th_unit = col("th_unit")
        nc.scalar.activation(th_unit[:], th_c[:], ACT.Copy, scale=1.0 / SPAN)
        bounded, gap, rest, near, far, ratio, power, z_unit, far_z = [
            col(name) for name in ("bounded", "gap", "rest", "near", "far", "ratio", "power", "z_unit", "far_z")
        ]
        p = sb.tile([P, I], F32, name="p")
        denominators = col("denominators", 2)
        z = denominators[:, 0:1]
        nc.scalar.activation(bounded[:], neg_max[:], ACT.Tanh, bias=th_unit[:], scale=1.0 / SPAN)
        nc.scalar.activation(gap[:], neg_max[:], ACT.Identity, bias=th_c[:])
        nc.scalar.activation(p[:], neg_a[:], ACT.Exp, bias=neg_max[:], scale=-1.0, accum_out=z)
        nc.scalar.activation(near[:], bounded[:], ACT.Exp, scale=-SPAN)
        steep_forms = col("steep_forms", 3, tag="neg_a_then_steep_forms")
        neg_steep, steep_less_one, neg_steep_unit = [steep_forms[:, n : n + 1] for n in range(3)]
        nc.scalar.activation(neg_steep, steep_c[:], ACT.Copy, scale=-1.0)
        nc.scalar.activation(ratio[:], z, ACT.Copy, scale=near[:])
        nc.gpsimd.tensor_tensor(power[:], ratio[:], neg_steep, ALU.pow)
        nc.scalar.activation(rest[:], bounded[:], ACT.Identity, bias=gap[:], scale=-SPAN)
        nc.scalar.activation(far[:], rest[:], ACT.Exp, scale=steep_c[:])
        nc.scalar.activation(z_unit[:], z, ACT.Copy, scale=1.0 / GRAD_SCALE)
        nc.scalar.activation(far_z[:], far[:], ACT.Copy, scale=z_unit[:])
        nc.scalar.activation(steep_less_one, steep_c[:], ACT.Copy, bias=-1.0)
        nc.scalar.activation(neg_steep_unit, steep_c[:], ACT.Copy, scale=-1.0 / GRAD_SCALE)
        nc.scalar.activation(denominators[:, 1:2], power[:], ACT.Identity, bias=z_unit[:], scale=far_z[:])

        v_picked = sb.tile([P, I], U16, name="v_picked", tag="picked_words", align_bytes=64)
        v_scale = sb.tile([P, I], U8, name="v_scale", tag="picked_bytes", align_bytes=64)
        nc.vector.tensor_copy(v_picked[:], v_words[:].indirect(offsets[:]))
        c_banks = [ps.tile([P, HALF], F32, name="c_bank%d" % h) for h in range(2)]
        for h in range(2):
            nc.vector.tensor_copy(v_scale[:, halves[h]], v_bytes[:].indirect(half_offsets[h]))
            product(c_banks[h][:], g_codes, g_block_scales, v_picked[:, halves[h]], v_scale[:, halves[h]])

        inv, base, slope, pull = col("inv", 2, tag="v_bytes_then_inv"), col("base"), col("slope"), col("pull")
        nc.vector.reciprocal(inv[:], denominators[:])
        inv_z, row_scale = inv[:, 0:1], inv[:, 1:2]
        nc.scalar.activation(base[:], inv_z, ACT.Copy, scale=steep_less_one)
        nc.scalar.activation(slope[:], row_scale, ACT.Identity, bias=base[:], scale=neg_steep_unit)

        own = sb.tile([P, I], F32, name="own")
        own_sums = col("own_sums", 2)
        own_scaled = sb.tile([P, I], F32, name="own_scaled")
        shared = sb.tile([P, I], F32, name="shared")
        for h in range(2):
            nc.vector.scalar_tensor_tensor(own[:, halves[h]], c_banks[h][:], kdot_c[:], p[:, halves[h]], ALU.subtract, ALU.mult, accum_out=own_sums[:, h : h + 1])
            nc.scalar.activation(own_scaled[:, halves[h]], own[:, halves[h]], ACT.Copy, scale=row_scale)
        nc.vector.tensor_scalar(pull[:], own_sums[:, 0:1], own_sums[:, 1:2], slope[:], ALU.add, ALU.mult)
        nc.vector.tensor_scalar(shared[:], p[:], pull[:], row_scale, ALU.mult, ALU.mult)
        nc.vector.tensor_tensor(placed[:].indirect(offsets[:]), own_scaled[:], shared[:], ALU.add)

        start = 0
        for n, width in enumerate(CHUNKS):
            cols = slice(start, start + width)
            total = sb.tile([P, width], F32, name="total%d" % n)
            nc.vector.tensor_tensor(total[:], placed[:, cols], old_sb[:, cols], ALU.add)
            nc.sync.dma_start(out[:, cols], total[:])
            start = start + width
